import numpy as np
import ml_dtypes


def mxq(x, axis, fmt="e4m3"):
    dtype, down = {"e4m3": (ml_dtypes.float8_e4m3fn, 7), "e5m2": (ml_dtypes.float8_e5m2, 14)}[fmt]
    v = np.moveaxis(np.asarray(x, np.float32).astype(ml_dtypes.bfloat16).astype(np.float64), axis, -1)
    blocks = v.reshape(v.shape[:-1] + (-1, 32))
    amax = np.abs(blocks).max(-1, keepdims=True)
    byte = np.maximum(np.where(amax > 0, np.frexp(amax)[1] - 1 + 127, 0) - down, 1)
    scale = np.exp2(byte - 127.0)
    codes = (blocks / scale).astype(np.float32).astype(dtype).astype(np.float64)
    return np.moveaxis((codes * scale).reshape(v.shape), -1, axis)


WIDE = False


def mx_kscale(k):
    if not WIDE:
        return np.ones(k)
    levels = np.array([10, -10, 5, -5, 0])
    if k % 512:
        return np.exp2(np.random.permutation(np.resize(levels, k // 32))).repeat(32)
    a = np.empty((k // 512, 16))
    for p in range(k // 512):
        a[p, :8] = np.random.permutation(np.resize(levels, 8))
        for g in range(8):
            far = levels[np.abs(levels - a[p, g]) >= 10]
            a[p, g + 8] = far[np.random.randint(len(far))]
    return np.exp2(a.ravel()).repeat(32)


def f64(x):
    return np.asarray(x).astype(np.float64)


def striped(idx):
    return np.tile(idx.reshape(-1, 16).T, (8, 1)).astype(np.uint16)


def unstriped(offs):
    return offs[:16].T.reshape(-1).astype(np.int64)


E2M1 = np.array([0.0, 0.5, 1.0, 1.5, 2.0, 3.0, 4.0, 6.0, -0.0, -0.5, -1.0, -1.5, -2.0, -3.0, -4.0, -6.0])


def pack_weight(w, fmt):
    k, n = w.shape
    w = f64(np.asarray(w, np.float32).astype(ml_dtypes.bfloat16)).reshape(k // 32, 32, n)
    amax = np.abs(w).max(1)
    if fmt == "e4m3":
        byte = np.frexp(amax)[1] - 1 + 127 - 7
    else:
        mant, ex = np.frexp(amax / 6.0)
        byte = np.where(mant > 0.5, ex, ex - 1) + 127
    byte = np.clip(np.where(amax > 0, byte, 1), 1, 254)
    scaled = (w * np.exp2(127.0 - byte)[:, None, :]).reshape(k, n).astype(np.float32)
    by_word = np.ascontiguousarray(scaled.reshape(k // 512, 128, 4, n).transpose(0, 1, 3, 2))
    if fmt == "e4m3":
        words = by_word.astype(ml_dtypes.float8_e4m3fn).view(np.uint8)
    else:
        c = by_word.astype(ml_dtypes.float4_e2m1fn).view(np.uint8) & 0xF
        words = (c[..., 0::2] | (c[..., 1::2] << 4)).reshape(k // 512, 128, 2 * n)
    return np.ascontiguousarray(words), np.ascontiguousarray(byte.astype(np.uint8).reshape(k // 512, 16, n))


def unpack_weight(words, scales, fmt):
    g, _, n = scales.shape
    words = np.ascontiguousarray(words).reshape(g, 128, n, -1)
    if fmt == "e4m3":
        vals = words.view(ml_dtypes.float8_e4m3fn).astype(np.float64)
    else:
        nib = np.empty((g, 128, n, 4), np.uint8)
        nib[..., 0::2] = words & 0xF
        nib[..., 1::2] = words >> 4
        vals = E2M1[nib]
    vals = vals * np.repeat(np.exp2(scales.astype(np.float64) - 127.0), 8, axis=1)[..., None]
    return vals.transpose(0, 1, 3, 2).reshape(g * 512, n)


def gelu(v):
    return 0.5 * v * (1.0 + np.tanh(np.sqrt(2.0 / np.pi) * (v + 0.044715 * v**3)))


def often(T, S):
    return np.random.permutation(T)[(T * np.random.uniform(0, 1, S) ** 4).astype(np.int64)]


K, M, T, S, P, H, N = 1024, 512, 2048, 1024, 512, 1024, 512

def setup_inputs():
    n = np.random.standard_normal
    s = mx_kscale(K)[:, None]
    s2 = mx_kscale(M)[:, None]
    u = mx_kscale(H)[:, None]
    d = {}
    d["tab_words"], d["tab_scales"] = pack_weight(n((K, T)) * s, "e4m3")
    d["tab2_words"], d["tab2_scales"] = pack_weight(n((M, T)) * s2, "e4m3")
    d["tab3_words"], d["tab3_scales"] = pack_weight(n((M, T)) * s2, "e4m3")
    d["offs"] = striped(np.random.permutation(T)[:S])
    d["offs2"] = striped(np.random.permutation(T)[:S])
    d["offs3"] = striped(np.random.permutation(T)[:S])
    d["pos1"] = striped(np.random.permutation(S)[:P])
    d["pos2"] = striped(often(S, P))
    d["pos3"] = striped(often(S, P))
    d["w1"] = (n((K, H)) / s * u.T / K ** 0.5).astype(np.float32)
    d["w2_words"], d["w2_scales"] = pack_weight(1.3 * n((M, H)) / s2 / M ** 0.5, "e2m1")
    d["bias2"] = (0.8 * n(H)).astype(np.float32)
    d["w3_words"], d["w3_scales"] = pack_weight(0.6 * n((M, H)) / s2 * u.T / M ** 0.5, "e4m3")
    d["w4_words"], d["w4_scales"] = pack_weight(1.2 * n((H, N)) / u / H ** 0.5, "e2m1")
    d["w5"] = (0.6 * n((H, N)) / u / H ** 0.5).astype(np.float32)
    d["bias5"] = (0.5 * n(N)).astype(np.float32)
    return d

def reference(tab_words, tab_scales, tab2_words, tab2_scales, tab3_words, tab3_scales, offs, offs2, offs3, pos1, pos2, pos3, w1, w2_words, w2_scales, bias2, w3_words, w3_scales, w4_words, w4_scales, w5, bias5):
    v = unpack_weight(tab_words, tab_scales, "e4m3")[:, unstriped(offs)]
    v2 = unpack_weight(tab2_words, tab2_scales, "e4m3")[:, unstriped(offs2)]
    v3 = unpack_weight(tab3_words, tab3_scales, "e4m3")[:, unstriped(offs3)]
    a = mxq(f64(w1), 0, "e4m3").T @ v
    b = (unpack_weight(w2_words, w2_scales, "e2m1").T @ v2) + f64(bias2)[:, None]
    d = unpack_weight(w3_words, w3_scales, "e4m3").T @ v3
    a1 = a[:, unstriped(pos1)]
    z = a1 / (1.0 + np.abs(b[:, unstriped(pos2)])) - d[:, unstriped(pos3)]
    zq = mxq(z, 0, "e4m3")
    aq = mxq(a1, 0, "e4m3")
    y = unpack_weight(w4_words, w4_scales, "e2m1").T @ zq + mxq(f64(w5), 0, "e4m3").T @ aq
    return y + f64(bias5)[:, None]

@@ -1,0 +1,300 @@
+from contextlib import ExitStack
+
+import concourse.mybir as mybir
+
+K, M, T, S, P, H, N = 1024, 512, 2048, 1024, 512, 1024, 512
+FLOPS = 2 * H * S * (K + M + M) + 2 * 2 * H * N * P
+
+F32 = mybir.dt.float32
+BF16 = mybir.dt.bfloat16
+I32 = mybir.dt.int32
+U32 = mybir.dt.uint32
+U16 = mybir.dt.uint16
+U8 = mybir.dt.uint8
+E4M3 = mybir.dt.float8_e4m3fn_x4
+E2M1 = mybir.dt.float4_e2m1fn_x4
+ACT = mybir.ActivationFunctionType
+ALU = mybir.AluOpType
+
+PARTS = 128
+BANK = 512
+
+
+def tile_list_crown_milling_join_kernel(
+    tc, tab_words, tab_scales, tab2_words, tab2_scales, tab3_words, tab3_scales,
+    offs, offs2, offs3, pos1, pos2, pos3, w1, w2_words, w2_scales, bias2,
+    w3_words, w3_scales, w4_words, w4_scales, w5, bias5, out,
+):
+    nc = tc.nc
+    with ExitStack() as ctx:
+        keep = ctx.enter_context(tc.tile_pool(name="keep", bufs=1))
+        ring = ctx.enter_context(tc.tile_pool(name="ring", bufs=2))
+        psum = ctx.enter_context(tc.psum_pool(name="psum", bufs=4))
+
+        def held(shape, dtype, name):
+            return keep.tile(shape, dtype, name=name, tag=name, align_bytes=64)
+
+        def load_list(src, name):
+            tile = keep.tile(list(src.shape), U16, name=name)
+            nc.sync.dma_start(tile[:], src)
+            return tile
+
+        def load_words(src, width, name):
+            tile = held([PARTS, width], I32, name)
+            nc.sync.dma_start(tile[:], src.bitcast(I32))
+            return tile
+
+        def zeroed_plane(width, name, engine):
+            tile = held([PARTS, width], U8, name)
+            engine.memset(tile[:].bitcast(I32), 0)
+            return tile
+
+        def load_scale_rows(queue, plane, scales, first):
+            passes = scales.shape[0]
+            for q in range(4):
+                row = 32 * q + first
+                queue.dma_start(
+                    plane[row : row + 4 * passes, :].bitcast(I32),
+                    scales[:, 4 * q : 4 * q + 4, :].bitcast(I32),
+                )
+
+        def gather(out_ap, window, offsets):
+            nc.vector.tensor_copy(out_ap, window.indirect(offsets[:]))
+
+        def table_words(src):
+            return src.rearrange("p n t -> p (n t)")
+
+        def gather_words(window, offsets, name):
+            picked = held([PARTS, S], U32, name)
+            gather(picked[:], window[:].bitcast(U32), offsets)
+            return picked
+
+        def gather_scales(window, offsets, name):
+            picked = held([PARTS, S], U8, name)
+            gather(picked[:], window[:], offsets)
+            return picked
+
+        def deal_columns(src, dtype, run, name):
+            dealt = held([PARTS, H], dtype, name)
+            nc.vector.tensor_copy(
+                dealt[:].rearrange("p (b t g m) -> p b g t m", b=2, t=4, m=run),
+                src.rearrange("p (b g m t) -> p b g t m", b=2, t=4, m=run),
+            )
+            return dealt
+
+        def load_rows(src, tag):
+            raw = keep.tile([PARTS, 4, BANK], F32, name=tag, tag=tag, align_bytes=64)
+            nc.sync.dma_start(raw[:], src.rearrange("(p j) c -> p j c", j=4))
+            return raw
+
+        def on_bytes_of(tag, name):
+            return keep.tile([PARTS, 4, P], F32, name=name, tag=tag, align_bytes=64)
+
+        banks_used = []
+
+        def quantise(grouped, name):
+            codes = held([PARTS, BANK], U32, name + "_codes")
+            plane = held([PARTS, BANK], U8, name + "_scales")
+            nc.vector.quantize_mx(out=codes[:].bitcast(E4M3), scales=plane[:], in_=grouped[:])
+            return codes, plane
+
+        def interleave(copy, planes, tag=None):
+            if tag:
+                grouped = keep.tile([PARTS, 4 * BANK], BF16, name=tag, tag=tag, align_bytes=64)
+            else:
+                grouped = ring.tile([PARTS, 4 * BANK], BF16, name="grouped", bufs=4, align_bytes=64)
+            copy(
+                grouped[:].rearrange("p (c i j) -> p c j i", i=4, j=4),
+                planes[:].rearrange("p j (c i) -> p c j i", i=4),
+            )
+            return grouped
+
+        def interleave_dealt(copy, planes, tag=None):
+            if tag:
+                grouped = keep.tile([PARTS, 4 * BANK], BF16, name=tag, tag=tag, align_bytes=64)
+            else:
+                grouped = ring.tile([PARTS, 4 * BANK], BF16, name="grouped", bufs=4, align_bytes=64)
+            copy(
+                grouped[:].rearrange("p (t m j) -> p m j t", t=4, j=4),
+                planes[:].rearrange("p j (m t) -> p m j t", t=4),
+            )
+            return grouped
+
+        def rows_tile(tag, bufs):
+            return ring.tile([PARTS, S], F32, name=tag, bufs=bufs)[:]
+
+        def first_stage(passes, window, empty):
+            for h in range(S // BANK):
+                cols = slice(BANK * h, BANK * (h + 1))
+                acc = psum.tile([PARTS, BANK], F32, name="acc", tag="acc%d" % (len(banks_used) % 4), bufs=1)
+                banks_used.append(acc)
+                for i, (lhs, lhs_scale, rhs, rhs_scale) in enumerate(passes):
+                    nc.tensor.matmul_mx(
+                        out=acc[:], lhsT=lhs, lhsT_scale=lhs_scale,
+                        rhs=rhs[:, cols].bitcast(E4M3), rhs_scale=rhs_scale[:, cols],
+                        start=(i == 0), stop=(i == len(passes) - 1),
+                    )
+                empty(window[:, cols], acc[:])
+            return window
+
+        def load_repeated_rows(scales, width, name):
+            plane = held([PARTS, width], U8, name)
+            for q in range(4):
+                rows = scales[0, 4 * q : 4 * q + 4, :].bitcast(I32)
+                nc.sync.dma_start(
+                    plane[32 * q : 32 * (q + 1), :].bitcast(I32),
+                    rows.unsqueeze(0).to_broadcast([8, 4, width // 4]),
+                )
+            return plane
+
+        tab_plane = zeroed_plane(T, "tab_plane", nc.vector)
+        tab3_plane = zeroed_plane(T, "tab3_plane", nc.vector)
+        w3_plane = zeroed_plane(H, "w3_plane", nc.vector)
+        w4_plane = zeroed_plane(2 * N, "w4_plane", nc.vector)
+
+        warm = held([PARTS, 2], F32, "warm")
+        nc.vector.memset(warm[:], 1.0)
+        nc.scalar.activation(warm[:, 1:2], warm[:, 0:1], ACT.Abs_reciprocal_sqrt)
+
+        offs2_t = load_list(offs2, "offs2_t")
+        tab2_plane = load_repeated_rows(tab2_scales, T, "tab2_plane")
+        w2_t = load_words(w2_words[0], H // 2, "w2_t")
+        tab2_t = load_words(table_words(tab2_words[0]), T, "tab2_t")
+        w2_plane = load_repeated_rows(w2_scales, H, "w2_plane")
+        offs_t = load_list(offs, "offs_t")
+        w1_raw = {}
+        w1_raw[0, 0] = load_rows(w1[0:512, 0:512], "raw_a")
+        load_scale_rows(nc.sync, tab_plane, tab_scales, 0)
+        bias2_t = held([PARTS, 2, 4], F32, "bias2_t")
+        nc.sync.dma_start(bias2_t[:], bias2.rearrange("(b p t) -> p b t", b=2, t=4))
+        pos2_t = load_list(pos2, "pos2_t")
+        tab_t = [load_words(table_words(tab_words[0]), T, "tab_t0")]
+        tab_t.append(load_words(table_words(tab_words[1]), T, "tab_t1"))
+        w1_raw[1, 0] = load_rows(w1[512:1024, 0:512], "raw_b")
+        w1_raw[0, 1] = load_rows(w1[0:512, 512:1024], "raw_c")
+        w1_raw[1, 1] = load_rows(w1[512:1024, 512:1024], "raw_d")
+        offs3_t = load_list(offs3, "offs3_t")
+        load_scale_rows(nc.sync, w3_plane, w3_scales, 0)
+        w3_t = load_words(table_words(w3_words[0]), H, "w3_t")
+        load_scale_rows(nc.sync, tab3_plane, tab3_scales, 0)
+        tab3_t = load_words(table_words(tab3_words[0]), T, "tab3_t")
+        pos1_t = load_list(pos1, "pos1_t")
+        pos3_t = load_list(pos3, "pos3_t")
+
+        def slice_cols(s):
+            return slice(PARTS * s, PARTS * (s + 1))
+
+        def blank_rows(s, window):
+            cols = slice_cols(s)
+            bias = bias2_t[:, s // 4, s % 4 : s % 4 + 1]
+            return first_stage(
+                [(w2_d[:, cols].bitcast(E2M1), w2_s[:, cols], v2, v2_scales)], window,
+                lambda dst, acc: nc.scalar.activation(dst, acc, ACT.Abs, bias=bias),
+            )
+
+        def bur_rows(s):
+            cols = slice_cols(s)
+            return first_stage(
+                [(w3_d[:, cols].bitcast(E4M3), w3_s[:, cols], v3, v3_scales)], rows_tile("d_rows", 6),
+                lambda dst, acc: nc.scalar.activation(dst, acc, ACT.Copy, scale=-1.0),
+            )
+
+        def scan_rows(s):
+            cols = slice_cols(s % 4)
+            passes = [
+                (w1_q[a, s // 4][0][:, cols].bitcast(E4M3), w1_q[a, s // 4][1][:, cols], v[a], v_scales[4 * a :, :])
+                for a in range(2)
+            ]
+            return first_stage(passes, rows_tile("a_rows", 4), nc.scalar.copy)
+
+        def pick_blanks(b, picked, tag):
+            pair = keep.tile([PARTS, 2, S], F32, name="b_pair", tag=tag, align_bytes=64)
+            for t in range(4):
+                window = pair[:, t, :] if t < 2 else rows_tile("b_rows", 2)
+                gather(picked[:, t, :], blank_rows(4 * b + t, window), pos2_t)
+
+        def damping(picked, factors):
+            for h in range(2):
+                pair = slice(2 * h, 2 * h + 2)
+                nc.scalar.activation(factors[:, pair, :], picked[:, pair, :], ACT.Abs_reciprocal_sqrt, bias=1.0)
+            for h in range(2):
+                pair = slice(2 * h, 2 * h + 2)
+                nc.scalar.activation(factors[:, pair, :], factors[:, pair, :], ACT.Square)
+
+        v2_scales = gather_scales(tab2_plane, offs2_t, "v2_scales")
+        w2_d = deal_columns(w2_t[:].bitcast(U16), U16, 8, "w2_d")
+        v2 = gather_words(tab2_t, offs2_t, "v2")
+        w2_s = deal_columns(w2_plane[:], U8, 16, "w2_s")
+        w1_q = {}
+        w1_q[0, 0] = quantise(interleave_dealt(nc.scalar.copy, w1_raw[0, 0]), "w1_00")
+        blanks = [on_bytes_of("tab2_t", "blanks0")]
+        pick_blanks(0, blanks[0], "raw_a")
+        v_scales = gather_scales(tab_plane, offs_t, "v_scales")
+        v = [gather_words(tab_t[a], offs_t, "v%d" % a) for a in range(2)]
+        w1_q[1, 0] = quantise(interleave_dealt(nc.scalar.copy, w1_raw[1, 0], "grouped_b"), "w1_10")
+        blanks.append(on_bytes_of("tab_t1", "blanks1"))
+        pick_blanks(1, blanks[1], "raw_b")
+        for a in range(2):
+            w1_q[a, 1] = quantise(interleave_dealt(nc.vector.tensor_copy, w1_raw[a, 1]), "w1_%d1" % a)
+        w3_s = deal_columns(w3_plane[:], U8, 16, "w3_s")
+        w3_d = deal_columns(w3_t[:].bitcast(U32), U32, 4, "w3_d")
+        v3_scales = gather_scales(tab3_plane, offs3_t, "v3_scales")
+        v3 = gather_words(tab3_t, offs3_t, "v3")
+
+        w5_raw = [load_rows(w5[512 * a : 512 * (a + 1), :], ("raw_a", "raw_c")[a]) for a in range(2)]
+        w4_t = held([PARTS, 2, N // 2], I32, "w4_t")
+        nc.sync.dma_start(w4_t[:], w4_words.bitcast(I32).rearrange("a p n -> p a n"))
+        for q in range(4):
+            nc.sync.dma_start(
+                w4_plane[32 * q : 32 * q + 4, :].bitcast(I32).rearrange("r (a n) -> r a n", a=2),
+                w4_scales[:, 4 * q : 4 * q + 4, :].bitcast(I32).rearrange("a r n -> r a n"),
+            )
+        bias5_t = held([PARTS, 4], F32, "bias5_t")
+        with nc.allow_non_contiguous_dma(reason="one bias value a partition"):
+            nc.sync.dma_start(bias5_t[:], bias5.rearrange("(i p) -> p i", p=PARTS))
+
+
+        def second_stage(lhs, lhs_scale, dtype, operand, start, stop):
+            for i in range(4):
+                cols = slice_cols(i)
+                nc.tensor.matmul_mx(
+                    out=acc_out[i][:], lhsT=lhs[:, cols].bitcast(dtype), lhsT_scale=lhs_scale[:, cols],
+                    rhs=operand[0][:].bitcast(E4M3), rhs_scale=operand[1][:], start=start, stop=stop,
+                )
+
+        factors = [on_bytes_of("grouped_b", "factors0"), on_bytes_of("tab_t0", "factors1")]
+        crowns = [on_bytes_of("tab3_t", "crowns0"), on_bytes_of("raw_d", "crowns1")]
+        joined = [on_bytes_of("tab2_t", "joined0"), on_bytes_of("tab_t1", "joined1")]
+        joined_q = []
+        for b in range(2):
+            a_rows = [scan_rows(4 * b + t) for t in range(4)]
+            if b == 0:
+                damping(blanks[0], factors[0])
+                damping(blanks[1], factors[1])
+            for t in range(4):
+                gather(crowns[b][:, t, :], a_rows[t], pos1_t)
+            for h in range(2):
+                pair = slice(2 * h, 2 * h + 2)
+                nc.vector.tensor_tensor(factors[b][:, pair, :], crowns[b][:, pair, :], factors[b][:, pair, :], ALU.mult)
+            for t in range(4):
+                d_rows = bur_rows(4 * b + t)
+                nc.vector.tensor_tensor(joined[b][:, t, :], d_rows.indirect(pos3_t[:]), factors[b][:, t, :], ALU.add)
+            if b == 0:
+                joined_q.append(quantise(interleave(nc.vector.tensor_copy, joined[0]), "joined_0"))
+        acc_out = [psum.tile([PARTS, P], F32, name="acc_out", tag="acc%d" % i, bufs=1) for i in range(4)]
+        for b in range(2):
+            w5_q = quantise(interleave(nc.scalar.copy, w5_raw[b]), "w5_%d" % b)
+            crowns_q = quantise(interleave(nc.scalar.copy, crowns[b], (None, "last")[b]), "crowns_%d" % b)
+            if b == 0:
+                second_stage(w4_t[:, 0, :].bitcast(U16), w4_plane[:, 0:N], E2M1, joined_q[0], True, False)
+            second_stage(w5_q[0], w5_q[1], E4M3, crowns_q, False, False)
+        joined_q.append(quantise(interleave(nc.vector.tensor_copy, joined[1], "last"), "joined_1"))
+        second_stage(w4_t[:, 1, :].bitcast(U16), w4_plane[:, N : 2 * N], E2M1, joined_q[1], False, True)
+
+        for i in range(4):
+            result = ring.tile([PARTS, P], F32, name="result", bufs=4)
+            if i % 2 == 0:
+                nc.scalar.activation(result[:], acc_out[i][:], ACT.Identity, bias=bias5_t[:, i : i + 1])
+            else:
+                nc.vector.tensor_scalar(result[:], acc_out[i][:], bias5_t[:, i : i + 1], None, ALU.add)
+            nc.sync.dma_start(out[slice_cols(i), :], result[:])

@@ -18,6 +18,7 @@ ALU = mybir.AluOpType
 
 PARTS = 128
 BANK = 512
+HALF = P // 2
 
 
 def tile_list_crown_milling_join_kernel(
@@ -93,8 +94,8 @@ def tile_list_crown_milling_join_kernel(
         banks_used = []
 
         def quantise(grouped, name):
-            codes = held([PARTS, BANK], U32, name + "_codes")
-            plane = held([PARTS, BANK], U8, name + "_scales")
+            codes = held([PARTS, grouped.shape[1] // 4], U32, name + "_codes")
+            plane = held([PARTS, grouped.shape[1] // 4], U8, name + "_scales")
             nc.vector.quantize_mx(out=codes[:].bitcast(E4M3), scales=plane[:], in_=grouped[:])
             return codes, plane
 
@@ -123,10 +124,16 @@ def tile_list_crown_milling_join_kernel(
         def rows_tile(tag, bufs):
             return ring.tile([PARTS, S], F32, name=tag, bufs=bufs)[:]
 
+        def gpsimd_cast(dst, src):
+            piece = dst.shape[1] // 4
+            for i in range(4):
+                part = slice(piece * i, piece * (i + 1))
+                nc.gpsimd.tensor_scalar(dst[:, part], src[:, part], 1.0, 0.0, ALU.mult, ALU.add)
+
         def first_stage(passes, window, empty):
             for h in range(S // BANK):
                 cols = slice(BANK * h, BANK * (h + 1))
-                acc = psum.tile([PARTS, BANK], F32, name="acc", tag="acc%d" % (len(banks_used) % 4), bufs=1)
+                acc = psum.tile([PARTS, BANK], F32, name="acc", tag="bank%d" % (len(banks_used) % 4 + (4 if len(banks_used) >= 44 else 0)), bufs=1)
                 banks_used.append(acc)
                 for i, (lhs, lhs_scale, rhs, rhs_scale) in enumerate(passes):
                     nc.tensor.matmul_mx(
@@ -235,13 +242,14 @@ def tile_list_crown_milling_join_kernel(
         blanks.append(on_bytes_of("tab_t1", "blanks1"))
         pick_blanks(1, blanks[1], "raw_b")
         for a in range(2):
-            w1_q[a, 1] = quantise(interleave_dealt(nc.vector.tensor_copy, w1_raw[a, 1]), "w1_%d1" % a)
+            w1_q[a, 1] = quantise(interleave_dealt(gpsimd_cast, w1_raw[a, 1]), "w1_%d1" % a)
         w3_s = deal_columns(w3_plane[:], U8, 16, "w3_s")
         w3_d = deal_columns(w3_t[:].bitcast(U32), U32, 4, "w3_d")
         v3_scales = gather_scales(tab3_plane, offs3_t, "v3_scales")
         v3 = gather_words(tab3_t, offs3_t, "v3")
 
         w5_raw = [load_rows(w5[512 * a : 512 * (a + 1), :], ("raw_a", "raw_c")[a]) for a in range(2)]
+        w5_q = [quantise(interleave(gpsimd_cast, w5_raw[a]), "w5_%d" % a) for a in range(2)]
         w4_t = held([PARTS, 2, N // 2], I32, "w4_t")
         nc.sync.dma_start(w4_t[:], w4_words.bitcast(I32).rearrange("a p n -> p a n"))
         for q in range(4):
@@ -254,47 +262,76 @@ def tile_list_crown_milling_join_kernel(
             nc.sync.dma_start(bias5_t[:], bias5.rearrange("(i p) -> p i", p=PARTS))
 
 
-        def second_stage(lhs, lhs_scale, dtype, operand, start, stop):
+        def second_stage(h, lhs, lhs_scale, dtype, operand, first, width, start, stop):
             for i in range(4):
                 cols = slice_cols(i)
-                nc.tensor.matmul_mx(
-                    out=acc_out[i][:], lhsT=lhs[:, cols].bitcast(dtype), lhsT_scale=lhs_scale[:, cols],
-                    rhs=operand[0][:].bitcast(E4M3), rhs_scale=operand[1][:], start=start, stop=stop,
-                )
+                for c in range(0, HALF, width):
+                    moving = slice(first + c, first + c + width)
+                    nc.tensor.matmul_mx(
+                        out=acc_out[h][i][:, c : c + width],
+                        lhsT=lhs[:, cols].bitcast(dtype), lhsT_scale=lhs_scale[:, cols],
+                        rhs=operand[0][:, moving].bitcast(E4M3), rhs_scale=operand[1][:, moving],
+                        start=start, stop=stop and c + width == HALF,
+                    )
+
+        def interleave_part(copy, grouped, planes, first, last):
+            copy(
+                grouped[:, 4 * first : 4 * last].rearrange("p (c i j) -> p c j i", i=4, j=4),
+                planes[:, :, first:last].rearrange("p j (c i) -> p c j i", i=4),
+            )
+
+        def pick_crowns(b, a_rows):
+            for t in range(4):
+                gather(crowns[b][:, t, :], a_rows[t], pos1_t)
 
         factors = [on_bytes_of("grouped_b", "factors0"), on_bytes_of("tab_t0", "factors1")]
         crowns = [on_bytes_of("tab3_t", "crowns0"), on_bytes_of("raw_d", "crowns1")]
-        joined = [on_bytes_of("tab2_t", "joined0"), on_bytes_of("tab_t1", "joined1")]
-        joined_q = []
-        for b in range(2):
-            a_rows = [scan_rows(4 * b + t) for t in range(4)]
-            if b == 0:
-                damping(blanks[0], factors[0])
-                damping(blanks[1], factors[1])
-            for t in range(4):
-                gather(crowns[b][:, t, :], a_rows[t], pos1_t)
-            for h in range(2):
-                pair = slice(2 * h, 2 * h + 2)
-                nc.vector.tensor_tensor(factors[b][:, pair, :], crowns[b][:, pair, :], factors[b][:, pair, :], ALU.mult)
-            for t in range(4):
-                d_rows = bur_rows(4 * b + t)
-                nc.vector.tensor_tensor(joined[b][:, t, :], d_rows.indirect(pos3_t[:]), factors[b][:, t, :], ALU.add)
-            if b == 0:
-                joined_q.append(quantise(interleave(nc.vector.tensor_copy, joined[0]), "joined_0"))
-        acc_out = [psum.tile([PARTS, P], F32, name="acc_out", tag="acc%d" % i, bufs=1) for i in range(4)]
-        for b in range(2):
-            w5_q = quantise(interleave(nc.scalar.copy, w5_raw[b]), "w5_%d" % b)
-            crowns_q = quantise(interleave(nc.scalar.copy, crowns[b], (None, "last")[b]), "crowns_%d" % b)
-            if b == 0:
-                second_stage(w4_t[:, 0, :].bitcast(U16), w4_plane[:, 0:N], E2M1, joined_q[0], True, False)
-            second_stage(w5_q[0], w5_q[1], E4M3, crowns_q, False, False)
-        joined_q.append(quantise(interleave(nc.vector.tensor_copy, joined[1], "last"), "joined_1"))
-        second_stage(w4_t[:, 1, :].bitcast(U16), w4_plane[:, N : 2 * N], E2M1, joined_q[1], False, True)
+        joined0 = on_bytes_of("tab2_t", "joined0")
 
-        for i in range(4):
-            result = ring.tile([PARTS, P], F32, name="result", bufs=4)
-            if i % 2 == 0:
-                nc.scalar.activation(result[:], acc_out[i][:], ACT.Identity, bias=bias5_t[:, i : i + 1])
-            else:
-                nc.vector.tensor_scalar(result[:], acc_out[i][:], bias5_t[:, i : i + 1], None, ALU.add)
-            nc.sync.dma_start(out[slice_cols(i), :], result[:])
+        a_rows = [scan_rows(t) for t in range(4)]
+        damping(blanks[0], factors[0])
+        damping(blanks[1], factors[1])
+        pick_crowns(0, a_rows)
+        for h in range(2):
+            pair = slice(2 * h, 2 * h + 2)
+            nc.vector.tensor_tensor(factors[0][:, pair, :], crowns[0][:, pair, :], factors[0][:, pair, :], ALU.mult)
+        for t in range(4):
+            nc.vector.tensor_tensor(joined0[:, t, :], bur_rows(t).indirect(pos3_t[:]), factors[0][:, t, :], ALU.add)
+        joined0_q = quantise(interleave(nc.vector.tensor_copy, joined0), "joined_0")
+
+        pick_crowns(1, [scan_rows(4 + t) for t in range(4)])
+        crowns_q = [quantise(interleave(nc.scalar.copy, crowns[0]), "crowns_0")]
+        for h in range(2):
+            pair = slice(2 * h, 2 * h + 2)
+            nc.vector.tensor_tensor(factors[1][:, pair, :], crowns[1][:, pair, :], factors[1][:, pair, :], ALU.mult)
+        d_rows = [bur_rows(4 + t) for t in range(4)]
+        crowns_q.append(quantise(interleave(nc.scalar.copy, crowns[1], "last"), "crowns_1"))
+
+        acc_out = [
+            [psum.tile([PARTS, HALF], F32, name="acc_out", tag="bank%d" % (4 * h + i), bufs=1) for i in range(4)]
+            for h in range(2)
+        ]
+        for h in range(2):
+            second_stage(h, w5_q[0][0], w5_q[0][1], E4M3, crowns_q[0], HALF * h, HALF, True, False)
+            second_stage(h, w4_t[:, 0, :].bitcast(U16), w4_plane[:, 0:N], E2M1, joined0_q, HALF * h, PARTS, False, False)
+        for h in range(2):
+            second_stage(h, w5_q[1][0], w5_q[1][1], E4M3, crowns_q[1], HALF * h, HALF, False, False)
+
+        for h in range(2):
+            cols = slice(HALF * h, HALF * (h + 1))
+            joined1 = keep.tile([PARTS, 4, HALF], F32, name="joined1", tag=("tab_t1", "last")[h], align_bytes=64)
+            for t in range(4):
+                nc.vector.tensor_tensor(
+                    joined1[:, t, :], d_rows[t].indirect(pos3_t[:, 16 * h : 16 * (h + 1)]), factors[1][:, t, cols], ALU.add
+                )
+            grouped = held([PARTS, 4 * HALF], BF16, "grouped_half%d" % h)
+            interleave_part((nc.scalar.copy, nc.vector.tensor_copy)[h], grouped, joined1, 0, HALF)
+            joined1_q = quantise(grouped, "joined_1%d" % h)
+            second_stage(h, w4_t[:, 1, :].bitcast(U16), w4_plane[:, N : 2 * N], E2M1, joined1_q, 0, PARTS, False, True)
+            for i in range(4):
+                result = ring.tile([PARTS, HALF], F32, name="result", bufs=8)
+                if h == 0 or i % 2 == 0:
+                    nc.scalar.activation(result[:], acc_out[h][i][:], ACT.Identity, bias=bias5_t[:, i : i + 1])
+                else:
+                    nc.vector.tensor_scalar(result[:], acc_out[h][i][:], bias5_t[:, i : i + 1], None, ALU.add)
+                nc.sync.dma_start(out[slice_cols(i), cols], result[:])

from contextlib import ExitStack

import concourse.mybir as mybir

K, M, T, S, P, H, N = 1024, 512, 2048, 1024, 512, 1024, 512
FLOPS = 2 * H * S * (K + M + M) + 2 * 2 * H * N * P

F32 = mybir.dt.float32
BF16 = mybir.dt.bfloat16
I32 = mybir.dt.int32
U32 = mybir.dt.uint32
U16 = mybir.dt.uint16
U8 = mybir.dt.uint8
E4M3 = mybir.dt.float8_e4m3fn_x4
E2M1 = mybir.dt.float4_e2m1fn_x4
ACT = mybir.ActivationFunctionType
ALU = mybir.AluOpType

PARTS = 128
BANK = 512
HALF = P // 2


def tile_list_crown_milling_join_kernel(
    tc, tab_words, tab_scales, tab2_words, tab2_scales, tab3_words, tab3_scales,
    offs, offs2, offs3, pos1, pos2, pos3, w1, w2_words, w2_scales, bias2,
    w3_words, w3_scales, w4_words, w4_scales, w5, bias5, out,
):
    nc = tc.nc
    with ExitStack() as ctx:
        keep = ctx.enter_context(tc.tile_pool(name="keep", bufs=1))
        ring = ctx.enter_context(tc.tile_pool(name="ring", bufs=2))
        psum = ctx.enter_context(tc.psum_pool(name="psum", bufs=4))

        def held(shape, dtype, name):
            return keep.tile(shape, dtype, name=name, tag=name, align_bytes=64)

        def load_list(src, name):
            tile = keep.tile(list(src.shape), U16, name=name)
            nc.sync.dma_start(tile[:], src)
            return tile

        def load_words(src, width, name):
            tile = held([PARTS, width], I32, name)
            nc.sync.dma_start(tile[:], src.bitcast(I32))
            return tile

        def zeroed_plane(width, name, engine):
            tile = held([PARTS, width], U8, name)
            engine.memset(tile[:].bitcast(I32), 0)
            return tile

        def load_scale_rows(queue, plane, scales, first):
            passes = scales.shape[0]
            for q in range(4):
                row = 32 * q + first
                queue.dma_start(
                    plane[row : row + 4 * passes, :].bitcast(I32),
                    scales[:, 4 * q : 4 * q + 4, :].bitcast(I32),
                )

        def gather(out_ap, window, offsets):
            nc.vector.tensor_copy(out_ap, window.indirect(offsets[:]))

        def table_words(src):
            return src.rearrange("p n t -> p (n t)")

        def gather_words(window, offsets, name):
            picked = held([PARTS, S], U32, name)
            gather(picked[:], window[:].bitcast(U32), offsets)
            return picked

        def gather_scales(window, offsets, name):
            picked = held([PARTS, S], U8, name)
            gather(picked[:], window[:], offsets)
            return picked

        def deal_columns(src, dtype, run, name):
            dealt = held([PARTS, H], dtype, name)
            nc.vector.tensor_copy(
                dealt[:].rearrange("p (b t g m) -> p b g t m", b=2, t=4, m=run),
                src.rearrange("p (b g m t) -> p b g t m", b=2, t=4, m=run),
            )
            return dealt

        def load_rows(src, tag):
            raw = keep.tile([PARTS, 4, BANK], F32, name=tag, tag=tag, align_bytes=64)
            nc.sync.dma_start(raw[:], src.rearrange("(p j) c -> p j c", j=4))
            return raw

        def on_bytes_of(tag, name):
            return keep.tile([PARTS, 4, P], F32, name=name, tag=tag, align_bytes=64)

        banks_used = []

        def quantise(grouped, name):
            codes = held([PARTS, grouped.shape[1] // 4], U32, name + "_codes")
            plane = held([PARTS, grouped.shape[1] // 4], U8, name + "_scales")
            nc.vector.quantize_mx(out=codes[:].bitcast(E4M3), scales=plane[:], in_=grouped[:])
            return codes, plane

        def interleave(copy, planes, tag=None):
            if tag:
                grouped = keep.tile([PARTS, 4 * BANK], BF16, name=tag, tag=tag, align_bytes=64)
            else:
                grouped = ring.tile([PARTS, 4 * BANK], BF16, name="grouped", bufs=4, align_bytes=64)
            copy(
                grouped[:].rearrange("p (c i j) -> p c j i", i=4, j=4),
                planes[:].rearrange("p j (c i) -> p c j i", i=4),
            )
            return grouped

        def interleave_dealt(copy, planes, tag=None):
            if tag:
                grouped = keep.tile([PARTS, 4 * BANK], BF16, name=tag, tag=tag, align_bytes=64)
            else:
                grouped = ring.tile([PARTS, 4 * BANK], BF16, name="grouped", bufs=4, align_bytes=64)
            copy(
                grouped[:].rearrange("p (t m j) -> p m j t", t=4, j=4),
                planes[:].rearrange("p j (m t) -> p m j t", t=4),
            )
            return grouped

        def rows_tile(tag, bufs):
            return ring.tile([PARTS, S], F32, name=tag, bufs=bufs)[:]

        def gpsimd_cast(dst, src):
            piece = dst.shape[1] // 4
            for i in range(4):
                part = slice(piece * i, piece * (i + 1))
                nc.gpsimd.tensor_scalar(dst[:, part], src[:, part], 1.0, 0.0, ALU.mult, ALU.add)

        def first_stage(passes, window, empty):
            for h in range(S // BANK):
                cols = slice(BANK * h, BANK * (h + 1))
                acc = psum.tile([PARTS, BANK], F32, name="acc", tag="bank%d" % (len(banks_used) % 4 + (4 if len(banks_used) >= 44 else 0)), bufs=1)
                banks_used.append(acc)
                for i, (lhs, lhs_scale, rhs, rhs_scale) in enumerate(passes):
                    nc.tensor.matmul_mx(
                        out=acc[:], lhsT=lhs, lhsT_scale=lhs_scale,
                        rhs=rhs[:, cols].bitcast(E4M3), rhs_scale=rhs_scale[:, cols],
                        start=(i == 0), stop=(i == len(passes) - 1),
                    )
                empty(window[:, cols], acc[:])
            return window

        def load_repeated_rows(scales, width, name):
            plane = held([PARTS, width], U8, name)
            for q in range(4):
                rows = scales[0, 4 * q : 4 * q + 4, :].bitcast(I32)
                nc.sync.dma_start(
                    plane[32 * q : 32 * (q + 1), :].bitcast(I32),
                    rows.unsqueeze(0).to_broadcast([8, 4, width // 4]),
                )
            return plane

        tab_plane = zeroed_plane(T, "tab_plane", nc.vector)
        tab3_plane = zeroed_plane(T, "tab3_plane", nc.vector)
        w3_plane = zeroed_plane(H, "w3_plane", nc.vector)
        w4_plane = zeroed_plane(2 * N, "w4_plane", nc.vector)

        warm = held([PARTS, 2], F32, "warm")
        nc.vector.memset(warm[:], 1.0)
        nc.scalar.activation(warm[:, 1:2], warm[:, 0:1], ACT.Abs_reciprocal_sqrt)

        offs2_t = load_list(offs2, "offs2_t")
        tab2_plane = load_repeated_rows(tab2_scales, T, "tab2_plane")
        w2_t = load_words(w2_words[0], H // 2, "w2_t")
        tab2_t = load_words(table_words(tab2_words[0]), T, "tab2_t")
        w2_plane = load_repeated_rows(w2_scales, H, "w2_plane")
        offs_t = load_list(offs, "offs_t")
        w1_raw = {}
        w1_raw[0, 0] = load_rows(w1[0:512, 0:512], "raw_a")
        load_scale_rows(nc.sync, tab_plane, tab_scales, 0)
        bias2_t = held([PARTS, 2, 4], F32, "bias2_t")
        nc.sync.dma_start(bias2_t[:], bias2.rearrange("(b p t) -> p b t", b=2, t=4))
        pos2_t = load_list(pos2, "pos2_t")
        tab_t = [load_words(table_words(tab_words[0]), T, "tab_t0")]
        tab_t.append(load_words(table_words(tab_words[1]), T, "tab_t1"))
        w1_raw[1, 0] = load_rows(w1[512:1024, 0:512], "raw_b")
        w1_raw[0, 1] = load_rows(w1[0:512, 512:1024], "raw_c")
        w1_raw[1, 1] = load_rows(w1[512:1024, 512:1024], "raw_d")
        offs3_t = load_list(offs3, "offs3_t")
        load_scale_rows(nc.sync, w3_plane, w3_scales, 0)
        w3_t = load_words(table_words(w3_words[0]), H, "w3_t")
        load_scale_rows(nc.sync, tab3_plane, tab3_scales, 0)
        tab3_t = load_words(table_words(tab3_words[0]), T, "tab3_t")
        pos1_t = load_list(pos1, "pos1_t")
        pos3_t = load_list(pos3, "pos3_t")

        def slice_cols(s):
            return slice(PARTS * s, PARTS * (s + 1))

        def blank_rows(s, window):
            cols = slice_cols(s)
            bias = bias2_t[:, s // 4, s % 4 : s % 4 + 1]
            return first_stage(
                [(w2_d[:, cols].bitcast(E2M1), w2_s[:, cols], v2, v2_scales)], window,
                lambda dst, acc: nc.scalar.activation(dst, acc, ACT.Abs, bias=bias),
            )

        def bur_rows(s):
            cols = slice_cols(s)
            return first_stage(
                [(w3_d[:, cols].bitcast(E4M3), w3_s[:, cols], v3, v3_scales)], rows_tile("d_rows", 6),
                lambda dst, acc: nc.scalar.activation(dst, acc, ACT.Copy, scale=-1.0),
            )

        def scan_rows(s):
            cols = slice_cols(s % 4)
            passes = [
                (w1_q[a, s // 4][0][:, cols].bitcast(E4M3), w1_q[a, s // 4][1][:, cols], v[a], v_scales[4 * a :, :])
                for a in range(2)
            ]
            return first_stage(passes, rows_tile("a_rows", 4), nc.scalar.copy)

        def pick_blanks(b, picked, tag):
            pair = keep.tile([PARTS, 2, S], F32, name="b_pair", tag=tag, align_bytes=64)
            for t in range(4):
                window = pair[:, t, :] if t < 2 else rows_tile("b_rows", 2)
                gather(picked[:, t, :], blank_rows(4 * b + t, window), pos2_t)

        def damping(picked, factors):
            for h in range(2):
                pair = slice(2 * h, 2 * h + 2)
                nc.scalar.activation(factors[:, pair, :], picked[:, pair, :], ACT.Abs_reciprocal_sqrt, bias=1.0)
            for h in range(2):
                pair = slice(2 * h, 2 * h + 2)
                nc.scalar.activation(factors[:, pair, :], factors[:, pair, :], ACT.Square)

        v2_scales = gather_scales(tab2_plane, offs2_t, "v2_scales")
        w2_d = deal_columns(w2_t[:].bitcast(U16), U16, 8, "w2_d")
        v2 = gather_words(tab2_t, offs2_t, "v2")
        w2_s = deal_columns(w2_plane[:], U8, 16, "w2_s")
        w1_q = {}
        w1_q[0, 0] = quantise(interleave_dealt(nc.scalar.copy, w1_raw[0, 0]), "w1_00")
        blanks = [on_bytes_of("tab2_t", "blanks0")]
        pick_blanks(0, blanks[0], "raw_a")
        v_scales = gather_scales(tab_plane, offs_t, "v_scales")
        v = [gather_words(tab_t[a], offs_t, "v%d" % a) for a in range(2)]
        w1_q[1, 0] = quantise(interleave_dealt(nc.scalar.copy, w1_raw[1, 0], "grouped_b"), "w1_10")
        blanks.append(on_bytes_of("tab_t1", "blanks1"))
        pick_blanks(1, blanks[1], "raw_b")
        for a in range(2):
            w1_q[a, 1] = quantise(interleave_dealt(gpsimd_cast, w1_raw[a, 1]), "w1_%d1" % a)
        w3_s = deal_columns(w3_plane[:], U8, 16, "w3_s")
        w3_d = deal_columns(w3_t[:].bitcast(U32), U32, 4, "w3_d")
        v3_scales = gather_scales(tab3_plane, offs3_t, "v3_scales")
        v3 = gather_words(tab3_t, offs3_t, "v3")

        w5_raw = [load_rows(w5[512 * a : 512 * (a + 1), :], ("raw_a", "raw_c")[a]) for a in range(2)]
        w5_q = [quantise(interleave(gpsimd_cast, w5_raw[a]), "w5_%d" % a) for a in range(2)]
        w4_t = held([PARTS, 2, N // 2], I32, "w4_t")
        nc.sync.dma_start(w4_t[:], w4_words.bitcast(I32).rearrange("a p n -> p a n"))
        for q in range(4):
            nc.sync.dma_start(
                w4_plane[32 * q : 32 * q + 4, :].bitcast(I32).rearrange("r (a n) -> r a n", a=2),
                w4_scales[:, 4 * q : 4 * q + 4, :].bitcast(I32).rearrange("a r n -> r a n"),
            )
        bias5_t = held([PARTS, 4], F32, "bias5_t")
        with nc.allow_non_contiguous_dma(reason="one bias value a partition"):
            nc.sync.dma_start(bias5_t[:], bias5.rearrange("(i p) -> p i", p=PARTS))


        def second_stage(h, lhs, lhs_scale, dtype, operand, first, width, start, stop):
            for i in range(4):
                cols = slice_cols(i)
                for c in range(0, HALF, width):
                    moving = slice(first + c, first + c + width)
                    nc.tensor.matmul_mx(
                        out=acc_out[h][i][:, c : c + width],
                        lhsT=lhs[:, cols].bitcast(dtype), lhsT_scale=lhs_scale[:, cols],
                        rhs=operand[0][:, moving].bitcast(E4M3), rhs_scale=operand[1][:, moving],
                        start=start, stop=stop and c + width == HALF,
                    )

        def interleave_part(copy, grouped, planes, first, last):
            copy(
                grouped[:, 4 * first : 4 * last].rearrange("p (c i j) -> p c j i", i=4, j=4),
                planes[:, :, first:last].rearrange("p j (c i) -> p c j i", i=4),
            )

        def pick_crowns(b, a_rows):
            for t in range(4):
                gather(crowns[b][:, t, :], a_rows[t], pos1_t)

        factors = [on_bytes_of("grouped_b", "factors0"), on_bytes_of("tab_t0", "factors1")]
        crowns = [on_bytes_of("tab3_t", "crowns0"), on_bytes_of("raw_d", "crowns1")]
        joined0 = on_bytes_of("tab2_t", "joined0")

        a_rows = [scan_rows(t) for t in range(4)]
        damping(blanks[0], factors[0])
        damping(blanks[1], factors[1])
        pick_crowns(0, a_rows)
        for h in range(2):
            pair = slice(2 * h, 2 * h + 2)
            nc.vector.tensor_tensor(factors[0][:, pair, :], crowns[0][:, pair, :], factors[0][:, pair, :], ALU.mult)
        for t in range(4):
            nc.vector.tensor_tensor(joined0[:, t, :], bur_rows(t).indirect(pos3_t[:]), factors[0][:, t, :], ALU.add)
        joined0_q = quantise(interleave(nc.vector.tensor_copy, joined0), "joined_0")

        pick_crowns(1, [scan_rows(4 + t) for t in range(4)])
        crowns_q = [quantise(interleave(nc.scalar.copy, crowns[0]), "crowns_0")]
        for h in range(2):
            pair = slice(2 * h, 2 * h + 2)
            nc.vector.tensor_tensor(factors[1][:, pair, :], crowns[1][:, pair, :], factors[1][:, pair, :], ALU.mult)
        d_rows = [bur_rows(4 + t) for t in range(4)]
        crowns_q.append(quantise(interleave(nc.scalar.copy, crowns[1], "last"), "crowns_1"))

        acc_out = [
            [psum.tile([PARTS, HALF], F32, name="acc_out", tag="bank%d" % (4 * h + i), bufs=1) for i in range(4)]
            for h in range(2)
        ]
        for h in range(2):
            second_stage(h, w5_q[0][0], w5_q[0][1], E4M3, crowns_q[0], HALF * h, HALF, True, False)
            second_stage(h, w4_t[:, 0, :].bitcast(U16), w4_plane[:, 0:N], E2M1, joined0_q, HALF * h, PARTS, False, False)
        for h in range(2):
            second_stage(h, w5_q[1][0], w5_q[1][1], E4M3, crowns_q[1], HALF * h, HALF, False, False)

        for h in range(2):
            cols = slice(HALF * h, HALF * (h + 1))
            joined1 = keep.tile([PARTS, 4, HALF], F32, name="joined1", tag=("tab_t1", "last")[h], align_bytes=64)
            for t in range(4):
                nc.vector.tensor_tensor(
                    joined1[:, t, :], d_rows[t].indirect(pos3_t[:, 16 * h : 16 * (h + 1)]), factors[1][:, t, cols], ALU.add
                )
            grouped = held([PARTS, 4 * HALF], BF16, "grouped_half%d" % h)
            interleave_part((nc.scalar.copy, nc.vector.tensor_copy)[h], grouped, joined1, 0, HALF)
            joined1_q = quantise(grouped, "joined_1%d" % h)
            second_stage(h, w4_t[:, 1, :].bitcast(U16), w4_plane[:, N : 2 * N], E2M1, joined1_q, 0, PARTS, False, True)
            for i in range(4):
                result = ring.tile([PARTS, HALF], F32, name="result", bufs=8)
                if h == 0 or i % 2 == 0:
                    nc.scalar.activation(result[:], acc_out[h][i][:], ACT.Identity, bias=bias5_t[:, i : i + 1])
                else:
                    nc.vector.tensor_scalar(result[:], acc_out[h][i][:], bias5_t[:, i : i + 1], None, ALU.add)
                nc.sync.dma_start(out[slice_cols(i), cols], result[:])
